import numpy as np
import ml_dtypes


def mxq(x, axis, fmt="e4m3"):
    dtype, down = {"e4m3": (ml_dtypes.float8_e4m3fn, 7), "e5m2": (ml_dtypes.float8_e5m2, 14)}[fmt]
    v = np.moveaxis(np.asarray(x, np.float32).astype(ml_dtypes.bfloat16).astype(np.float64), axis, -1)
    blocks = v.reshape(v.shape[:-1] + (-1, 32))
    amax = np.abs(blocks).max(-1, keepdims=True)
    byte = np.maximum(np.where(amax > 0, np.frexp(amax)[1] - 1 + 127, 0) - down, 1)
    scale = np.exp2(byte - 127.0)
    codes = (blocks / scale).astype(np.float32).astype(dtype).astype(np.float64)
    return np.moveaxis((codes * scale).reshape(v.shape), -1, axis)


WIDE = False


def mx_kscale(k):
    if not WIDE:
        return np.ones(k)
    levels = np.array([10, -10, 5, -5, 0])
    if k % 512:
        return np.exp2(np.random.permutation(np.resize(levels, k // 32))).repeat(32)
    a = np.empty((k // 512, 16))
    for p in range(k // 512):
        a[p, :8] = np.random.permutation(np.resize(levels, 8))
        for g in range(8):
            far = levels[np.abs(levels - a[p, g]) >= 10]
            a[p, g + 8] = far[np.random.randint(len(far))]
    return np.exp2(a.ravel()).repeat(32)


def f64(x):
    return np.asarray(x).astype(np.float64)


def striped(idx):
    return np.tile(idx.reshape(-1, 16).T, (8, 1)).astype(np.uint16)


def unstriped(offs):
    return offs[:16].T.reshape(-1).astype(np.int64)


def pack_weight(w):
    k, n = w.shape
    w = f64(np.asarray(w, np.float32).astype(ml_dtypes.bfloat16)).reshape(k // 32, 32, n)
    amax = np.abs(w).max(1)
    byte = np.clip(np.where(amax > 0, np.frexp(amax)[1] - 1 + 127 - 7, 1), 1, 254)
    scaled = (w * np.exp2(127.0 - byte)[:, None, :]).reshape(k, n).astype(np.float32)
    words = np.ascontiguousarray(scaled.reshape(k // 512, 128, 4, n).transpose(0, 1, 3, 2)).astype(ml_dtypes.float8_e4m3fn).view(np.uint8)
    return words, np.ascontiguousarray(byte.astype(np.uint8).reshape(k // 512, 16, n))


def unpack_weight(words, scales):
    g, p, n, _ = words.shape
    vals = np.ascontiguousarray(words).view(ml_dtypes.float8_e4m3fn).astype(np.float64) * np.repeat(np.exp2(scales.astype(np.float64) - 127.0), 8, axis=1)[..., None]
    return vals.transpose(0, 1, 3, 2).reshape(g * 512, n)


K, T, S, N, V = 1024, 1024, 512, 256, 256
P = 2 ** 7


def setup_inputs():
    n = np.random.standard_normal
    s = mx_kscale(K)[:, None]
    near = np.random.permutation(S)
    packed_xT = pack_weight(n((K, T)) * s)
    return {
        "x_words": packed_xT[0],
        "x_scales": packed_xT[1],
        "w1": (n((K, N)) / np.sqrt(K) / s).astype(np.float32),
        "beta": (np.tile(np.random.uniform(0.2, 1.5, S), (P, 1))).astype(np.float32),
        "pmax": (np.tile(np.random.uniform(0.7, 1.0, V), (P, 1))).astype(np.float32),
        "offs": striped(np.random.permutation(T)[:S]),
        "ra": striped(near[:V]),
        "rb": striped(near[V:]),
    }


def reference(x_words, x_scales, w1, beta, pmax, offs, ra, rb):
    xq = unpack_weight(x_words, x_scales)[:, unstriped(offs)]
    y = mxq(f64(w1), 0, "e4m3").T @ xq
    ener = (y) ** 2 + 0.5 * np.abs(y)
    ea = ener[:, unstriped(ra)]
    eb = ener[:, unstriped(rb)]
    dlt = (f64(beta)[:1][:, unstriped(ra)] - (f64(beta)[:1][:, unstriped(rb)])) * (ea - eb)
    return np.minimum(np.exp(dlt), f64(pmax)[:1])

@@ -1,0 +1,105 @@
+from contextlib import ExitStack
+
+import concourse.mybir as mybir
+
+K, T, S, N, V = 1024, 1024, 512, 256, 256
+FLOPS = 2 * K * N * S
+
+F32 = mybir.dt.float32
+BF16 = mybir.dt.bfloat16
+I32 = mybir.dt.int32
+U32 = mybir.dt.uint32
+U16 = mybir.dt.uint16
+U8 = mybir.dt.uint8
+FP8X4 = mybir.dt.float8_e4m3fn_x4
+ACT = mybir.ActivationFunctionType
+ALU = mybir.AluOpType
+
+P = 128
+PACK = 4
+PASSES = K // (P * PACK)
+BLOCKS = N // P
+QUADS = 4
+
+
+def tile_picked_ytempr_acc_p_kernel(tc, x_words, x_scales, w1, beta, pmax, offs, ra, rb, out):
+    nc = tc.nc
+    with ExitStack() as ctx:
+        sb = ctx.enter_context(tc.tile_pool(name="sb", bufs=1))
+        psum = ctx.enter_context(tc.psum_pool(name="psum", bufs=1))
+
+        offs_t = sb.tile([P, S // 16], U16, name="offs_t")
+        ra_t = sb.tile([P, V // 16], U16, name="ra_t")
+        rb_t = sb.tile([P, V // 16], U16, name="rb_t")
+        xw = [sb.tile([P, T], U32, name="xw%d" % o, align_bytes=64) for o in range(PASSES)]
+        xs = sb.tile([P, T], U8, name="xs", align_bytes=64)
+        wraw = [sb.tile([P, PACK, N], F32, name="wraw%d" % o) for o in range(PASSES)]
+        beta_t = sb.tile([P, S], F32, name="beta_t")
+        pmax_t = sb.tile([P, V], F32, name="pmax_t")
+
+        nc.vector.memset(xs[:].bitcast(I32), 0)
+        for q in range(QUADS):
+            nc.scalar.dma_start(out=xs[32 * q:32 * q + 4 * PASSES, :].bitcast(I32),
+                                in_=x_scales[:, 4 * q:4 * q + 4, :].bitcast(I32))
+        nc.sync.dma_start(offs_t[:], offs)
+        for o in range(PASSES):
+            nc.sync.dma_start(out=xw[o][:].bitcast(I32),
+                              in_=x_words[o].rearrange("p n t -> p (n t)").bitcast(I32))
+        for o in range(PASSES):
+            nc.sync.dma_start(out=wraw[o][:],
+                              in_=w1[o * 512:(o + 1) * 512, :].rearrange("(p j) n -> p j n", j=PACK))
+        nc.sync.dma_start(ra_t[:], ra)
+        nc.sync.dma_start(rb_t[:], rb)
+        nc.sync.dma_start(out=beta_t[:], in_=beta)
+        nc.sync.dma_start(out=pmax_t[:], in_=pmax)
+
+        gs = sb.tile([P, S], U8, name="gs", align_bytes=64)
+        nc.vector.tensor_copy(gs[:], xs[:].indirect(offs_t[:]))
+        gw = []
+        for o in range(PASSES):
+            g = sb.tile([P, S], U32, name="gw%d" % o, align_bytes=64)
+            nc.vector.tensor_copy(g[:], xw[o][:].indirect(offs_t[:]))
+            gw.append(g)
+
+        def quantise(o, b, on_vector):
+            grouped = sb.tile([P, P * PACK], BF16, name="wb%d%d" % (o, b), align_bytes=64)
+            dst = grouped[:].rearrange("p (c i t) -> p c t i", i=4, t=PACK)
+            src = wraw[o][:, :, b * P:(b + 1) * P].rearrange("p t (c i) -> p c t i", i=4)
+            if on_vector:
+                nc.vector.tensor_copy(out=dst, in_=src)
+            else:
+                nc.scalar.activation(out=dst, in_=src, func=ACT.Copy)
+            codes = sb.tile([P, P], U32, name="wc%d%d" % (o, b), align_bytes=64)
+            scales = sb.tile([P, P], U8, name="ws%d%d" % (o, b), align_bytes=64)
+            nc.vector.quantize_mx(out=codes[:].bitcast(FP8X4), scales=scales[:], in_=grouped[:])
+            return codes, scales
+
+        y = [psum.tile([P, S], F32, name="y%d" % b) for b in range(BLOCKS)]
+        for o in range(PASSES):
+            for b in range(BLOCKS):
+                codes, scales = quantise(o, b, (o, b) == (1, 0))
+                nc.tensor.matmul_mx(out=y[b][:], lhsT=codes[:].bitcast(FP8X4), lhsT_scale=scales[:],
+                                    rhs=gw[o][:].bitcast(FP8X4), rhs_scale=gs[4 * o:P, :],
+                                    start=(o == 0), stop=(o == PASSES - 1))
+
+        ba = sb.tile([P, V], F32, name="ba")
+        db = sb.tile([P, V], F32, name="db")
+        nc.vector.tensor_copy(ba[:], beta_t[:].indirect(ra_t[:]))
+        nc.vector.tensor_tensor(db[:], beta_t[:].indirect(rb_t[:]), ba[:], ALU.subtract)
+
+        for b in range(BLOCKS):
+            mag = sb.tile([P, S], F32, name="mag%d" % b)
+            en = sb.tile([P, S], F32, name="en%d" % b)
+            nc.scalar.activation(out=mag[:], in_=y[b][:], func=ACT.Abs)
+            nc.scalar.activation(out=en[:], in_=mag[:], func=ACT.Square, bias=0.25)
+            ea = sb.tile([P, V], F32, name="ea%d" % b)
+            de = sb.tile([P, V], F32, name="de%d" % b)
+            dl = sb.tile([P, V], F32, name="dl%d" % b)
+            ex = sb.tile([P, V], F32, name="ex%d" % b)
+            res = sb.tile([P, V], F32, name="res%d" % b)
+            nc.vector.tensor_copy(ea[:], en[:].indirect(ra_t[:]))
+            nc.vector.tensor_tensor(de[:], en[:].indirect(rb_t[:]), ea[:], ALU.subtract)
+            nc.vector.tensor_tensor(dl[:], de[:], db[:], ALU.mult)
+            nc.scalar.activation(out=ex[:], in_=dl[:], func=ACT.Exp)
+            nc.vector.tensor_tensor(res[:], ex[:], pmax_t[:], ALU.min)
+            nc.sync.dma_start(out=out[b * P:(b + 1) * P, :], in_=res[:])

@@ -1,6 +1,7 @@
 from contextlib import ExitStack
 
 import concourse.mybir as mybir
+from concourse.masks import make_identity
 
 K, T, S, N, V = 1024, 1024, 512, 256, 256
 FLOPS = 2 * K * N * S
@@ -20,6 +21,7 @@ PACK = 4
 PASSES = K // (P * PACK)
 BLOCKS = N // P
 QUADS = 4
+PIECES = [[(0, 256), (256, 384), (384, 512)], [(0, 256), (256, 512)]]
 
 
 def tile_picked_ytempr_acc_p_kernel(tc, x_words, x_scales, w1, beta, pmax, offs, ra, rb, out):
@@ -31,75 +33,134 @@ def tile_picked_ytempr_acc_p_kernel(tc, x_words, x_scales, w1, beta, pmax, offs,
         offs_t = sb.tile([P, S // 16], U16, name="offs_t")
         ra_t = sb.tile([P, V // 16], U16, name="ra_t")
         rb_t = sb.tile([P, V // 16], U16, name="rb_t")
-        xw = [sb.tile([P, T], U32, name="xw%d" % o, align_bytes=64) for o in range(PASSES)]
+        xw = [sb.tile([P, T], U32, name="xw%d" % o, tag="xw%d" % o, align_bytes=64) for o in range(PASSES)]
+        xs_in = sb.tile([P, T], U8, name="xs_in", align_bytes=64)
         xs = sb.tile([P, T], U8, name="xs", align_bytes=64)
-        wraw = [sb.tile([P, PACK, N], F32, name="wraw%d" % o) for o in range(PASSES)]
+        w_raw = [sb.tile([P, PACK, N], F32, name="w_raw%d" % o) for o in range(PASSES)]
         beta_t = sb.tile([P, S], F32, name="beta_t")
+        beta_in = sb.tile([P, S // P], F32, name="beta_in", tag="wb00", align_bytes=64)
         pmax_t = sb.tile([P, V], F32, name="pmax_t")
+        ident = sb.tile([P, P], F32, name="ident", tag="wb01", align_bytes=64)
+        zero = sb.tile([P, 1], F32, name="zero")
+        quarter = sb.tile([P, 1], F32, name="quarter")
 
+        nc.gpsimd.memset(zero[:], 0.0)
+        nc.scalar.activation(out=quarter[:], in_=zero[:], func=ACT.Identity, bias=0.25)
         nc.vector.memset(xs[:].bitcast(I32), 0)
-        for q in range(QUADS):
-            nc.scalar.dma_start(out=xs[32 * q:32 * q + 4 * PASSES, :].bitcast(I32),
-                                in_=x_scales[:, 4 * q:4 * q + 4, :].bitcast(I32))
-        nc.sync.dma_start(offs_t[:], offs)
-        for o in range(PASSES):
+        make_identity(nc, ident[:])
+
+        def load_words(o):
             nc.sync.dma_start(out=xw[o][:].bitcast(I32),
                               in_=x_words[o].rearrange("p n t -> p (n t)").bitcast(I32))
-        for o in range(PASSES):
-            nc.sync.dma_start(out=wraw[o][:],
-                              in_=w1[o * 512:(o + 1) * 512, :].rearrange("(p j) n -> p j n", j=PACK))
+
+        w_rows = w1.rearrange("(o p j) n -> o p j n", o=PASSES, j=PACK)
+        nc.sync.dma_start(out=beta_in[:], in_=beta[0, :].rearrange("(p c) -> p c", p=P))
+        for q in range(QUADS):
+            nc.sync.dma_start(out=xs_in[32 * q:32 * q + 4 * PASSES, :].bitcast(I32),
+                              in_=x_scales[:, 4 * q:4 * q + 4, :].bitcast(I32))
+        nc.sync.dma_start(offs_t[:], offs)
+        load_words(0)
+        nc.sync.dma_start(out=w_raw[0][:], in_=w_rows[0])
         nc.sync.dma_start(ra_t[:], ra)
         nc.sync.dma_start(rb_t[:], rb)
-        nc.sync.dma_start(out=beta_t[:], in_=beta)
+        nc.sync.dma_start(out=w_raw[1][:], in_=w_rows[1])
+        load_words(1)
         nc.sync.dma_start(out=pmax_t[:], in_=pmax)
 
+        beta_ps = psum.tile([P, S // P, P], F32, name="beta_ps")
+        for c in range(S // P):
+            nc.tensor.transpose(beta_ps[:, c, :], beta_in[:, c:c + 1].to_broadcast([P, P]), ident[:])
+        nc.scalar.copy(beta_t[:].rearrange("p (n c) -> p n c", c=S // P), beta_ps[:].rearrange("p c n -> p n c"))
+        for q in range(QUADS):
+            rows = slice(32 * q, 32 * q + 4 * PASSES)
+            nc.vector.tensor_copy(xs[rows, :].bitcast(I32), xs_in[rows, :].bitcast(I32))
         gs = sb.tile([P, S], U8, name="gs", align_bytes=64)
         nc.vector.tensor_copy(gs[:], xs[:].indirect(offs_t[:]))
-        gw = []
-        for o in range(PASSES):
-            g = sb.tile([P, S], U32, name="gw%d" % o, align_bytes=64)
-            nc.vector.tensor_copy(g[:], xw[o][:].indirect(offs_t[:]))
-            gw.append(g)
+        gw = [sb.tile([P, S], U32, name="gw0", align_bytes=64)]
+        nc.vector.tensor_copy(gw[0][:], xw[0][:].indirect(offs_t[:]))
 
-        def quantise(o, b, on_vector):
-            grouped = sb.tile([P, P * PACK], BF16, name="wb%d%d" % (o, b), align_bytes=64)
+        def rounded(o, b):
+            label = "%d%d" % (o, b)
+            grouped = sb.tile([P, P * PACK], BF16, name="wb" + label, tag="wb" + label, align_bytes=64)
             dst = grouped[:].rearrange("p (c i t) -> p c t i", i=4, t=PACK)
-            src = wraw[o][:, :, b * P:(b + 1) * P].rearrange("p t (c i) -> p c t i", i=4)
-            if on_vector:
-                nc.vector.tensor_copy(out=dst, in_=src)
-            else:
-                nc.scalar.activation(out=dst, in_=src, func=ACT.Copy)
-            codes = sb.tile([P, P], U32, name="wc%d%d" % (o, b), align_bytes=64)
-            scales = sb.tile([P, P], U8, name="ws%d%d" % (o, b), align_bytes=64)
+            src = w_raw[o][:, :, b * P:(b + 1) * P].rearrange("p t (c i) -> p c t i", i=4)
+            nc.scalar.activation(out=dst, in_=src, func=ACT.Copy)
+            return grouped
+
+        def quantise(o, b, grouped, tag):
+            label = "%d%d" % (o, b)
+            codes = sb.tile([P, P], U32, name="wc" + label, tag=tag, align_bytes=64)
+            scales = sb.tile([P, P], U8, name="ws" + label, align_bytes=64)
             nc.vector.quantize_mx(out=codes[:].bitcast(FP8X4), scales=scales[:], in_=grouped[:])
             return codes, scales
 
-        y = [psum.tile([P, S], F32, name="y%d" % b) for b in range(BLOCKS)]
-        for o in range(PASSES):
-            for b in range(BLOCKS):
-                codes, scales = quantise(o, b, (o, b) == (1, 0))
-                nc.tensor.matmul_mx(out=y[b][:], lhsT=codes[:].bitcast(FP8X4), lhsT_scale=scales[:],
-                                    rhs=gw[o][:].bitcast(FP8X4), rhs_scale=gs[4 * o:P, :],
-                                    start=(o == 0), stop=(o == PASSES - 1))
-
+        wq = {(0, b): quantise(0, b, rounded(0, b), "wc0%d" % b) for b in range(BLOCKS)}
         ba = sb.tile([P, V], F32, name="ba")
-        db = sb.tile([P, V], F32, name="db")
         nc.vector.tensor_copy(ba[:], beta_t[:].indirect(ra_t[:]))
-        nc.vector.tensor_tensor(db[:], beta_t[:].indirect(rb_t[:]), ba[:], ALU.subtract)
+        wq[(1, 0)] = quantise(1, 0, rounded(1, 0), "wc10")
+        last_rounded = rounded(1, 1)
+        gw.append(sb.tile([P, S], U32, name="gw1", tag="wb10", align_bytes=64))
+
+        y = [[psum.tile([P, hi - lo], F32, name="y%d_%d" % (b, lo), tag="y%d_%d" % (b, lo))
+              for lo, hi in PIECES[b]] for b in range(BLOCKS)]
+
+        def product(o, b, i):
+            lo, hi = PIECES[b][i]
+            codes, scales = wq[(o, b)]
+            nc.tensor.matmul_mx(out=y[b][i][:], lhsT=codes[:].bitcast(FP8X4), lhsT_scale=scales[:],
+                                rhs=gw[o][:, lo:hi].bitcast(FP8X4), rhs_scale=gs[4 * o:P, lo:hi],
+                                start=(o == 0), stop=(o == PASSES - 1))
 
         for b in range(BLOCKS):
-            mag = sb.tile([P, S], F32, name="mag%d" % b)
-            en = sb.tile([P, S], F32, name="en%d" % b)
-            nc.scalar.activation(out=mag[:], in_=y[b][:], func=ACT.Abs)
-            nc.scalar.activation(out=en[:], in_=mag[:], func=ACT.Square, bias=0.25)
+            for i in range(len(PIECES[b])):
+                product(0, b, i)
+        for i, (lo, hi) in enumerate(PIECES[0]):
+            nc.vector.tensor_copy(gw[1][:, lo:hi], xw[1][:].indirect(offs_t[:, lo // 16:hi // 16]))
+            product(1, 0, i)
+        wq[(1, 1)] = quantise(1, 1, last_rounded, "xw1")
+        db = sb.tile([P, V], F32, name="db", tag="wc10", align_bytes=64)
+        nc.vector.tensor_tensor(db[:], beta_t[:].indirect(rb_t[:]), ba[:], ALU.subtract)
+        for i in range(len(PIECES[1])):
+            product(1, 1, i)
+
+        en = []
+        for b in range(BLOCKS):
+            mag = sb.tile([P, S], F32, name="mag%d" % b, tag="mag")
+            sq = sb.tile([P, S], F32, name="en%d" % b)
+            for i, (lo, hi) in enumerate(PIECES[b]):
+                nc.scalar.activation(out=mag[:, lo:hi], in_=y[b][i][:], func=ACT.Abs)
+            for lo, hi in PIECES[b]:
+                nc.scalar.activation(out=sq[:, lo:hi], in_=mag[:, lo:hi], func=ACT.Square, bias=quarter[:])
+            en.append(sq)
+
+        def fetch_a(b):
             ea = sb.tile([P, V], F32, name="ea%d" % b)
-            de = sb.tile([P, V], F32, name="de%d" % b)
-            dl = sb.tile([P, V], F32, name="dl%d" % b)
-            ex = sb.tile([P, V], F32, name="ex%d" % b)
-            res = sb.tile([P, V], F32, name="res%d" % b)
-            nc.vector.tensor_copy(ea[:], en[:].indirect(ra_t[:]))
-            nc.vector.tensor_tensor(de[:], en[:].indirect(rb_t[:]), ea[:], ALU.subtract)
-            nc.vector.tensor_tensor(dl[:], de[:], db[:], ALU.mult)
+            nc.vector.tensor_copy(ea[:], en[b][:].indirect(ra_t[:]))
+            return ea
+
+        def fetch_b(b, ea, lo, hi):
+            de = sb.tile([P, hi - lo], F32, name="de%d_%d" % (b, lo))
+            nc.vector.tensor_tensor(de[:], en[b][:].indirect(rb_t[:, lo // 16:hi // 16]), ea[:, lo:hi], ALU.subtract)
+            return de
+
+        def chance(b, de, lo, hi, tag):
+            dl = sb.tile([P, hi - lo], F32, name="dl%d_%d" % (b, lo), tag=tag)
+            ex = sb.tile([P, hi - lo], F32, name="ex%d_%d" % (b, lo))
+            nc.vector.tensor_tensor(dl[:], de[:], db[:, lo:hi], ALU.mult)
             nc.scalar.activation(out=ex[:], in_=dl[:], func=ACT.Exp)
-            nc.vector.tensor_tensor(res[:], ex[:], pmax_t[:], ALU.min)
-            nc.sync.dma_start(out=out[b * P:(b + 1) * P, :], in_=res[:])
+            return ex
+
+        def cap(b, ex, lo, hi):
+            res = sb.tile([P, hi - lo], F32, name="res%d_%d" % (b, lo))
+            nc.vector.tensor_tensor(res[:], ex[:], pmax_t[:, lo:hi], ALU.min)
+            nc.sync.dma_start(out=out[b * P:(b + 1) * P, lo:hi], in_=res[:])
+
+        de0 = fetch_b(0, fetch_a(0), 0, V)
+        ea1 = fetch_a(1)
+        ex0 = chance(0, de0, 0, V, "mag")
+        halves = [(0, V // 2), (V // 2, V)]
+        de1 = [fetch_b(1, ea1, lo, hi) for lo, hi in halves]
+        ex1 = [chance(1, de, lo, hi, "dl1_%d" % lo) for de, (lo, hi) in zip(de1, halves)]
+        cap(0, ex0, 0, V)
+        for ex, (lo, hi) in zip(ex1, halves):
+            cap(1, ex, lo, hi)

from contextlib import ExitStack

import concourse.mybir as mybir
from concourse.masks import make_identity

K, T, S, N, V = 1024, 1024, 512, 256, 256
FLOPS = 2 * K * N * S

F32 = mybir.dt.float32
BF16 = mybir.dt.bfloat16
I32 = mybir.dt.int32
U32 = mybir.dt.uint32
U16 = mybir.dt.uint16
U8 = mybir.dt.uint8
FP8X4 = mybir.dt.float8_e4m3fn_x4
ACT = mybir.ActivationFunctionType
ALU = mybir.AluOpType

P = 128
PACK = 4
PASSES = K // (P * PACK)
BLOCKS = N // P
QUADS = 4
PIECES = [[(0, 256), (256, 384), (384, 512)], [(0, 256), (256, 512)]]


def tile_picked_ytempr_acc_p_kernel(tc, x_words, x_scales, w1, beta, pmax, offs, ra, rb, out):
    nc = tc.nc
    with ExitStack() as ctx:
        sb = ctx.enter_context(tc.tile_pool(name="sb", bufs=1))
        psum = ctx.enter_context(tc.psum_pool(name="psum", bufs=1))

        offs_t = sb.tile([P, S // 16], U16, name="offs_t")
        ra_t = sb.tile([P, V // 16], U16, name="ra_t")
        rb_t = sb.tile([P, V // 16], U16, name="rb_t")
        xw = [sb.tile([P, T], U32, name="xw%d" % o, tag="xw%d" % o, align_bytes=64) for o in range(PASSES)]
        xs_in = sb.tile([P, T], U8, name="xs_in", align_bytes=64)
        xs = sb.tile([P, T], U8, name="xs", align_bytes=64)
        w_raw = [sb.tile([P, PACK, N], F32, name="w_raw%d" % o) for o in range(PASSES)]
        beta_t = sb.tile([P, S], F32, name="beta_t")
        beta_in = sb.tile([P, S // P], F32, name="beta_in", tag="wb00", align_bytes=64)
        pmax_t = sb.tile([P, V], F32, name="pmax_t")
        ident = sb.tile([P, P], F32, name="ident", tag="wb01", align_bytes=64)
        zero = sb.tile([P, 1], F32, name="zero")
        quarter = sb.tile([P, 1], F32, name="quarter")

        nc.gpsimd.memset(zero[:], 0.0)
        nc.scalar.activation(out=quarter[:], in_=zero[:], func=ACT.Identity, bias=0.25)
        nc.vector.memset(xs[:].bitcast(I32), 0)
        make_identity(nc, ident[:])

        def load_words(o):
            nc.sync.dma_start(out=xw[o][:].bitcast(I32),
                              in_=x_words[o].rearrange("p n t -> p (n t)").bitcast(I32))

        w_rows = w1.rearrange("(o p j) n -> o p j n", o=PASSES, j=PACK)
        nc.sync.dma_start(out=beta_in[:], in_=beta[0, :].rearrange("(p c) -> p c", p=P))
        for q in range(QUADS):
            nc.sync.dma_start(out=xs_in[32 * q:32 * q + 4 * PASSES, :].bitcast(I32),
                              in_=x_scales[:, 4 * q:4 * q + 4, :].bitcast(I32))
        nc.sync.dma_start(offs_t[:], offs)
        load_words(0)
        nc.sync.dma_start(out=w_raw[0][:], in_=w_rows[0])
        nc.sync.dma_start(ra_t[:], ra)
        nc.sync.dma_start(rb_t[:], rb)
        nc.sync.dma_start(out=w_raw[1][:], in_=w_rows[1])
        load_words(1)
        nc.sync.dma_start(out=pmax_t[:], in_=pmax)

        beta_ps = psum.tile([P, S // P, P], F32, name="beta_ps")
        for c in range(S // P):
            nc.tensor.transpose(beta_ps[:, c, :], beta_in[:, c:c + 1].to_broadcast([P, P]), ident[:])
        nc.scalar.copy(beta_t[:].rearrange("p (n c) -> p n c", c=S // P), beta_ps[:].rearrange("p c n -> p n c"))
        for q in range(QUADS):
            rows = slice(32 * q, 32 * q + 4 * PASSES)
            nc.vector.tensor_copy(xs[rows, :].bitcast(I32), xs_in[rows, :].bitcast(I32))
        gs = sb.tile([P, S], U8, name="gs", align_bytes=64)
        nc.vector.tensor_copy(gs[:], xs[:].indirect(offs_t[:]))
        gw = [sb.tile([P, S], U32, name="gw0", align_bytes=64)]
        nc.vector.tensor_copy(gw[0][:], xw[0][:].indirect(offs_t[:]))

        def rounded(o, b):
            label = "%d%d" % (o, b)
            grouped = sb.tile([P, P * PACK], BF16, name="wb" + label, tag="wb" + label, align_bytes=64)
            dst = grouped[:].rearrange("p (c i t) -> p c t i", i=4, t=PACK)
            src = w_raw[o][:, :, b * P:(b + 1) * P].rearrange("p t (c i) -> p c t i", i=4)
            nc.scalar.activation(out=dst, in_=src, func=ACT.Copy)
            return grouped

        def quantise(o, b, grouped, tag):
            label = "%d%d" % (o, b)
            codes = sb.tile([P, P], U32, name="wc" + label, tag=tag, align_bytes=64)
            scales = sb.tile([P, P], U8, name="ws" + label, align_bytes=64)
            nc.vector.quantize_mx(out=codes[:].bitcast(FP8X4), scales=scales[:], in_=grouped[:])
            return codes, scales

        wq = {(0, b): quantise(0, b, rounded(0, b), "wc0%d" % b) for b in range(BLOCKS)}
        ba = sb.tile([P, V], F32, name="ba")
        nc.vector.tensor_copy(ba[:], beta_t[:].indirect(ra_t[:]))
        wq[(1, 0)] = quantise(1, 0, rounded(1, 0), "wc10")
        last_rounded = rounded(1, 1)
        gw.append(sb.tile([P, S], U32, name="gw1", tag="wb10", align_bytes=64))

        y = [[psum.tile([P, hi - lo], F32, name="y%d_%d" % (b, lo), tag="y%d_%d" % (b, lo))
              for lo, hi in PIECES[b]] for b in range(BLOCKS)]

        def product(o, b, i):
            lo, hi = PIECES[b][i]
            codes, scales = wq[(o, b)]
            nc.tensor.matmul_mx(out=y[b][i][:], lhsT=codes[:].bitcast(FP8X4), lhsT_scale=scales[:],
                                rhs=gw[o][:, lo:hi].bitcast(FP8X4), rhs_scale=gs[4 * o:P, lo:hi],
                                start=(o == 0), stop=(o == PASSES - 1))

        for b in range(BLOCKS):
            for i in range(len(PIECES[b])):
                product(0, b, i)
        for i, (lo, hi) in enumerate(PIECES[0]):
            nc.vector.tensor_copy(gw[1][:, lo:hi], xw[1][:].indirect(offs_t[:, lo // 16:hi // 16]))
            product(1, 0, i)
        wq[(1, 1)] = quantise(1, 1, last_rounded, "xw1")
        db = sb.tile([P, V], F32, name="db", tag="wc10", align_bytes=64)
        nc.vector.tensor_tensor(db[:], beta_t[:].indirect(rb_t[:]), ba[:], ALU.subtract)
        for i in range(len(PIECES[1])):
            product(1, 1, i)

        en = []
        for b in range(BLOCKS):
            mag = sb.tile([P, S], F32, name="mag%d" % b, tag="mag")
            sq = sb.tile([P, S], F32, name="en%d" % b)
            for i, (lo, hi) in enumerate(PIECES[b]):
                nc.scalar.activation(out=mag[:, lo:hi], in_=y[b][i][:], func=ACT.Abs)
            for lo, hi in PIECES[b]:
                nc.scalar.activation(out=sq[:, lo:hi], in_=mag[:, lo:hi], func=ACT.Square, bias=quarter[:])
            en.append(sq)

        def fetch_a(b):
            ea = sb.tile([P, V], F32, name="ea%d" % b)
            nc.vector.tensor_copy(ea[:], en[b][:].indirect(ra_t[:]))
            return ea

        def fetch_b(b, ea, lo, hi):
            de = sb.tile([P, hi - lo], F32, name="de%d_%d" % (b, lo))
            nc.vector.tensor_tensor(de[:], en[b][:].indirect(rb_t[:, lo // 16:hi // 16]), ea[:, lo:hi], ALU.subtract)
            return de

        def chance(b, de, lo, hi, tag):
            dl = sb.tile([P, hi - lo], F32, name="dl%d_%d" % (b, lo), tag=tag)
            ex = sb.tile([P, hi - lo], F32, name="ex%d_%d" % (b, lo))
            nc.vector.tensor_tensor(dl[:], de[:], db[:, lo:hi], ALU.mult)
            nc.scalar.activation(out=ex[:], in_=dl[:], func=ACT.Exp)
            return ex

        def cap(b, ex, lo, hi):
            res = sb.tile([P, hi - lo], F32, name="res%d_%d" % (b, lo))
            nc.vector.tensor_tensor(res[:], ex[:], pmax_t[:, lo:hi], ALU.min)
            nc.sync.dma_start(out=out[b * P:(b + 1) * P, lo:hi], in_=res[:])

        de0 = fetch_b(0, fetch_a(0), 0, V)
        ea1 = fetch_a(1)
        ex0 = chance(0, de0, 0, V, "mag")
        halves = [(0, V // 2), (V // 2, V)]
        de1 = [fetch_b(1, ea1, lo, hi) for lo, hi in halves]
        ex1 = [chance(1, de, lo, hi, "dl1_%d" % lo) for de, (lo, hi) in zip(de1, halves)]
        cap(0, ex0, 0, V)
        for ex, (lo, hi) in zip(ex1, halves):
            cap(1, ex, lo, hi)
